import numpy as np
import ml_dtypes


def mxq(x, axis, fmt="e4m3"):
    dtype, down = {"e4m3": (ml_dtypes.float8_e4m3fn, 7), "e5m2": (ml_dtypes.float8_e5m2, 14)}[fmt]
    v = np.moveaxis(np.asarray(x, np.float32).astype(ml_dtypes.bfloat16).astype(np.float64), axis, -1)
    blocks = v.reshape(v.shape[:-1] + (-1, 32))
    amax = np.abs(blocks).max(-1, keepdims=True)
    byte = np.maximum(np.where(amax > 0, np.frexp(amax)[1] - 1 + 127, 0) - down, 1)
    scale = np.exp2(byte - 127.0)
    codes = (blocks / scale).astype(np.float32).astype(dtype).astype(np.float64)
    return np.moveaxis((codes * scale).reshape(v.shape), -1, axis)


WIDE = False


def mx_kscale(k):
    if not WIDE:
        return np.ones(k)
    levels = np.array([10, -10, 5, -5, 0])
    if k % 512:
        return np.exp2(np.random.permutation(np.resize(levels, k // 32))).repeat(32)
    a = np.empty((k // 512, 16))
    for p in range(k // 512):
        a[p, :8] = np.random.permutation(np.resize(levels, 8))
        for g in range(8):
            far = levels[np.abs(levels - a[p, g]) >= 10]
            a[p, g + 8] = far[np.random.randint(len(far))]
    return np.exp2(a.ravel()).repeat(32)


def f64(x):
    return np.asarray(x).astype(np.float64)


def striped(idx):
    return np.tile(np.asarray(idx).reshape(-1, 16).T, (8, 1)).astype(np.uint16)


def unstriped(offs):
    return offs[:16].T.reshape(-1).astype(np.int64)

def rot(x):
    y = x.reshape(x.shape[0], -1, 2, x.shape[2])
    return np.stack([-y[:, :, 1], y[:, :, 0]], axis=2).reshape(x.shape)


B, N, T, D, NQ = 1, 512, 2048, 512, 256
DV = 512


def sgn(shape):
    return np.random.uniform(0.5, 2.0, shape) * np.where(np.random.standard_normal(shape) < 0, -1.0, 1.0)


def setup_inputs():
    n = np.random.standard_normal
    idx = np.random.permutation(T)[:B * N]
    idx2 = np.random.permutation(1024)[:B * N]
    s = mx_kscale(D)[:, None]
    u = mx_kscale(N)
    ut = np.ones(T)
    ut[idx] = u
    return {
        "qT": (n((B, D, NQ)) * s * (1.00 / np.sqrt(D))).astype(np.float32),
        "kT": (np.clip(np.round(n((D, T)) * 16), -64, 64) / 16 / s).astype(np.float32),
        "cT": (np.repeat(np.round(np.cos(np.arange(D // 2)[:, None] * 0.11 + np.arange(1024)[None] * 0.37) * 64) / 64, 2, axis=0)).astype(np.float32),
        "wT": (np.repeat(np.round(np.sin(np.arange(D // 2)[:, None] * 0.11 + np.arange(1024)[None] * 0.37) * 64) / 64, 2, axis=0)).astype(np.float32),
        "vT": (n((DV, T)) / ut).astype(np.float32),
        "ls": (np.random.uniform(7.0, 7.6, (B, 1, NQ))).astype(np.float32),
        "us": (sgn((B, N, 1)) * u[:, None]).astype(np.float32),
        "offs": striped(idx),
        "offs2": striped(idx2),
    }


def reference(qT, kT, cT, wT, vT, ls, us, offs, offs2):
    idx = unstriped(offs)
    idx2 = unstriped(offs2)
    pick = lambda x, which: x[:, which].reshape(x.shape[0], B, -1).transpose(1, 0, 2)
    kg = pick(f64(kT), idx)
    cg = pick(f64(cT), idx2)
    wg = pick(f64(wT), idx2)
    ug = mxq(kg * cg + rot(kg) * wg, 1, "e4m3")
    qq = mxq(f64(qT), 1, "e4m3")
    a = ug.transpose(0, 2, 1) @ qq
    y = np.exp(a - f64(ls)) * f64(us)
    wq = mxq(y, 1, "e4m3")
    o = wq.transpose(0, 2, 1) @ mxq(pick(f64(vT), idx).transpose(0, 2, 1), 1, "e4m3")
    return o

@@ -1,0 +1,182 @@
+from contextlib import ExitStack
+
+import concourse.mybir as mybir
+from concourse.masks import make_identity
+
+D, NQ, T, TP, N, DV = 512, 256, 2048, 1024, 512, 512
+FLOPS = 2 * D * N * NQ + 2 * N * NQ * DV
+BYTES = 4 * (D * NQ + D * T + D * TP + DV * T + NQ + N + NQ * DV) + 2 * 2 * 128 * (N // 16)
+
+F32 = mybir.dt.float32
+BF16 = mybir.dt.bfloat16
+U32 = mybir.dt.uint32
+U16 = mybir.dt.uint16
+U8 = mybir.dt.uint8
+FP8X4 = mybir.dt.float8_e4m3fn_x4
+ACT = mybir.ActivationFunctionType
+ALU = mybir.AluOpType
+
+P = 128
+PACK = 4
+QB = NQ // P
+VB = DV // P
+HALF = N // 2
+
+
+def tile_attend_at_rope_f_topk_kernel(tc, qT, kT, cT, wT, vT, ls, us, offs, offs2, out):
+    nc = tc.nc
+    with ExitStack() as ctx:
+        sb = ctx.enter_context(tc.tile_pool(name="sb", bufs=1))
+        ps = ctx.enter_context(tc.psum_pool(name="ps", bufs=1))
+
+        def load(name, shape, dtype, src, tag=""):
+            tile = sb.tile(shape, dtype, name=name, tag=tag, align_bytes=64)
+            nc.sync.dma_start(out=tile[:], in_=src)
+            return tile
+
+        def quantize(name, source, tag=""):
+            words = source.shape[1] // PACK
+            codes = sb.tile([P, words], U32, name=name + "_codes", tag=tag, align_bytes=64)
+            scales = sb.tile([P, words], U8, name=name + "_scales", align_bytes=64)
+            nc.vector.quantize_mx(codes[:].bitcast(FP8X4), scales[:], source)
+            return codes, scales
+
+        k_rows = kT.rearrange("(p t) n -> p t n", t=PACK)
+        c_rows = cT.rearrange("(p t) n -> p t n", t=PACK)
+        w_rows = wT.rearrange("(p t) n -> p t n", t=PACK)
+
+        pos_list = load("pos_list", [P, N // 16], U16, offs2)
+        cos, sin = [], []
+        for h in range(2):
+            cos.append(load("cos%d" % h, [P, TP], F32, c_rows[:, 2 * h, :]))
+            sin.append(load("sin%d" % h, [P, TP], F32, w_rows[:, 2 * h, :]))
+        tok_list = load("tok_list", [P, N // 16], U16, offs)
+        keys = [load("key%d" % t, [P, T], F32, k_rows[:, t, :]) for t in range(PACK)]
+        q_raw = load("q_raw", [P, PACK, NQ], F32, qT[0].rearrange("(p t) q -> p t q", t=PACK))
+        lse = load("lse", [P, QB], F32, ls[0, 0].rearrange("(p b) -> p b", b=QB))
+        slot_scale = load("slot_scale", [P, PACK], F32, us[0].rearrange("(s r) o -> s (r o)", r=PACK))
+        values = [load("value%d" % j, [P, T], F32, vT[j * P : (j + 1) * P, :], tag="value%d" % j) for j in range(VB)]
+
+        ident = sb.tile([P, P], F32, name="ident")
+        make_identity(nc, ident[:])
+
+        warm = sb.tile([P, 1], F32, name="warm")
+        nc.scalar.activation(warm[:], ident[:, 0:1], ACT.Exp)
+
+        trig = []
+        for h in range(2):
+            tile = sb.tile([P, 3, N], F32, name="trig%d" % h)
+            nc.vector.tensor_copy(tile[:, 1, :], cos[h][:].indirect(pos_list[:]))
+            nc.vector.tensor_copy(tile[:, 2, :], sin[h][:].indirect(pos_list[:]))
+            nc.scalar.mul(tile[:, 0, :], tile[:, 2, :], -1.0)
+            trig.append(tile)
+
+        def products(t):
+            h, odd = divmod(t, 2)
+            picked = [sb.tile([P, HALF], F32, name="picked%d_%d" % (t, g)) for g in range(2)]
+            terms = [sb.tile([P, 2, HALF], F32, name="terms%d_%d" % (t, g)) for g in range(2)]
+            for g in range(2):
+                nc.vector.tensor_copy(picked[g][:], keys[t][:].indirect(tok_list[:, g * HALF // 16 : (g + 1) * HALF // 16]))
+            for g in range(2):
+                factors = trig[h][:, 1 - odd : 3 - odd, g * HALF : (g + 1) * HALF]
+                nc.vector.tensor_tensor(terms[g][:], factors, picked[g][:].unsqueeze(1).broadcast_to([P, 2, HALF]), ALU.mult)
+            return terms
+
+        pairs = [sb.tile([P, 2, HALF], F32, name="pairs%d" % g) for g in range(2)]
+
+        even, odd = products(0), products(1)
+        back = ps.tile([P, 2, HALF], F32, name="back", tag="turned", bufs=2)
+        for g in range(2):
+            sums = ps.tile([P, 2, 2, P], F32, name="sums", tag="wide", bufs=2)
+            for c in range(2):
+                for t in range(2):
+                    cols = slice(c * P, (c + 1) * P)
+                    nc.tensor.matmul(sums[:, c, t, :], even[g][:, t, cols], ident[:], start=True, stop=False, is_transpose=True)
+                    nc.tensor.matmul(sums[:, c, t, :], odd[g][:, t, cols], ident[:], start=False, stop=True, is_transpose=True)
+            rounded = sb.tile([P, 2, P, 2], BF16, name="rounded%d" % g)
+            nc.scalar.copy(rounded[:], sums[:].rearrange("s c t p -> s c p t"))
+            rounded_words = rounded[:].rearrange("s c p t -> s (c p t)").bitcast(F32)
+            for c in range(2):
+                nc.tensor.transpose(back[:, g, c * P : (c + 1) * P], rounded_words[:, c * P : (c + 1) * P], ident[:])
+        for g in range(2):
+            nc.scalar.copy(pairs[g][:, 0, :], back[:, g, :])
+
+        even, odd = products(2), products(3)
+        for g in range(2):
+            nc.vector.tensor_tensor(
+                pairs[g][:, 1, :].bitcast(BF16).rearrange("p (c i t) -> p c t i", i=4, t=2),
+                even[g][:].rearrange("p t (c i) -> p c t i", i=4),
+                odd[g][:].rearrange("p t (c i) -> p c t i", i=4),
+                ALU.add,
+            )
+
+        q_grouped = sb.tile([P, QB, P, PACK], BF16, name="q_grouped", align_bytes=64)
+        nc.scalar.copy(q_grouped[:], q_raw[:].rearrange("p t (m b) -> p b m t", b=QB))
+        neg_lse = sb.tile([P, QB], F32, name="neg_lse")
+        nc.scalar.mul(neg_lse[:], lse[:], -1.0)
+        q_codes, q_scales = quantize("q", q_grouped[:].rearrange("p b m t -> p (b m t)"))
+
+        u_mx = []
+        for g in range(2):
+            u = sb.tile([P, HALF, 2], F32, name="u%d" % g, tag="u%d" % g, align_bytes=64)
+            nc.scalar.copy(u[:], pairs[g][:].rearrange("p h s -> p s h"))
+            u_mx.append(quantize("u%d" % g, u[:].rearrange("p s h -> p (s h)").bitcast(BF16)))
+
+        scores = [ps.tile([P, N], F32, name="scores%d" % b, tag="wide", bufs=2) for b in range(QB)]
+        for g in range(2):
+            for b in range(QB):
+                cols = slice(b * P, (b + 1) * P)
+                nc.tensor.matmul_mx(scores[b][:, g * HALF : (g + 1) * HALF], q_codes[:, cols].bitcast(FP8X4), q_scales[:, cols],
+                                    u_mx[g][0][:].bitcast(FP8X4), u_mx[g][1][:], start=True, stop=True)
+
+        y = sb.tile([P, QB, P, PACK], BF16, name="y", tag="value1", align_bytes=64)
+        turned = []
+        for b in range(QB):
+            e = sb.tile([P, PACK, P], F32, name="e%d" % b)
+            nc.scalar.activation(e[:], scores[b][:].rearrange("p (s r) -> p r s", r=PACK), ACT.Exp, bias=neg_lse[:, b : b + 1])
+            e_t = ps.tile([P, PACK, P], F32, name="e_t%d" % b, tag="turned", bufs=2)
+            for r in range(PACK):
+                nc.tensor.transpose(e_t[:, r, :], e[:, r, :], ident[:])
+            turned.append(e_t)
+
+        def turn_values(j, tag, grouped):
+            vg = sb.tile([P, N], BF16, name="vg%d" % j, tag=tag, align_bytes=64)
+            nc.vector.tensor_copy(vg[:], values[j][:].indirect(tok_list[:]))
+            words = vg[:].bitcast(F32)
+            v_t = ps.tile([P, 2, P], F32, name="v_t", bufs=2)
+            for h in range(2):
+                nc.tensor.transpose(v_t[:, h, :], words[:, h : N // 2 : 2], ident[:])
+            nc.scalar.copy(grouped.rearrange("p (e h) -> p e h", h=2), v_t[:].rearrange("p h e -> p e h"))
+
+        out_rows = out[0].rearrange("(p b) e -> p b e", b=QB)
+
+        def multiply(j, codes, scales):
+            acc = ps.tile([P, QB, P], F32, name="acc", bufs=2)
+            for b in range(QB):
+                cols = slice(b * P, (b + 1) * P)
+                nc.tensor.matmul_mx(acc[:, b, :], y_codes[:, cols].bitcast(FP8X4), y_scales[:, cols],
+                                    codes.bitcast(FP8X4), scales, start=True, stop=True)
+            result = sb.tile([P, QB, P], F32, name="result%d" % j)
+            nc.scalar.copy(result[:], acc[:])
+            nc.sync.dma_start(out=out_rows[:, :, j * P : (j + 1) * P], in_=result[:])
+
+        v01 = sb.tile([P, 2 * 2 * P], F32, name="v01", align_bytes=64)
+        turn_values(0, "u1", v01[:, 0 : 2 * P])
+        turn_values(1, "", v01[:, 2 * P : 4 * P])
+
+        for b in range(QB):
+            nc.vector.tensor_tensor(y[:, b], turned[b][:].rearrange("p r q -> p q r"),
+                                    slot_scale[:].unsqueeze(1).broadcast_to([P, P, PACK]), ALU.mult)
+        v_codes, v_scales = quantize("v01", v01[:].bitcast(BF16))
+        y_codes, y_scales = quantize("y", y[:].rearrange("p b q r -> p (b q r)"))
+        for j in range(2):
+            multiply(j, v_codes[:, j * P : (j + 1) * P], v_scales[:, j * P : (j + 1) * P])
+
+        v2 = sb.tile([P, 2 * P], F32, name="v2", align_bytes=64)
+        v3 = sb.tile([P, 2 * P], F32, name="v3", align_bytes=64)
+        turn_values(2, "value1", v2[:])
+        turn_values(3, "", v3[:])
+        v_codes, v_scales = quantize("v2", v2[:].bitcast(BF16), tag="value3")
+        multiply(2, v_codes[:], v_scales[:])
+        v_codes, v_scales = quantize("v3", v3[:].bitcast(BF16))
+        multiply(3, v_codes[:], v_scales[:])

@@ -34,9 +34,10 @@ def tile_attend_at_rope_f_topk_kernel(tc, qT, kT, cT, wT, vT, ls, us, offs, offs
             nc.sync.dma_start(out=tile[:], in_=src)
             return tile
 
-        def quantize(name, source, tag=""):
+        def quantize(name, source, codes=None):
             words = source.shape[1] // PACK
-            codes = sb.tile([P, words], U32, name=name + "_codes", tag=tag, align_bytes=64)
+            if codes is None:
+                codes = sb.tile([P, words], U32, name=name + "_codes", align_bytes=64)
             scales = sb.tile([P, words], U8, name=name + "_scales", align_bytes=64)
             nc.vector.quantize_mx(codes[:].bitcast(FP8X4), scales[:], source)
             return codes, scales
@@ -116,11 +117,10 @@ def tile_attend_at_rope_f_topk_kernel(tc, qT, kT, cT, wT, vT, ls, us, offs, offs
         nc.scalar.mul(neg_lse[:], lse[:], -1.0)
         q_codes, q_scales = quantize("q", q_grouped[:].rearrange("p b m t -> p (b m t)"))
 
-        u_mx = []
-        for g in range(2):
-            u = sb.tile([P, HALF, 2], F32, name="u%d" % g, tag="u%d" % g, align_bytes=64)
-            nc.scalar.copy(u[:], pairs[g][:].rearrange("p h s -> p s h"))
-            u_mx.append(quantize("u%d" % g, u[:].rearrange("p s h -> p (s h)").bitcast(BF16)))
+        u = [sb.tile([P, HALF, 2], F32, name="u%d" % g, align_bytes=64) for g in range(2)]
+        nc.scalar.copy(u[0][:], pairs[0][:].rearrange("p h s -> p s h"))
+        nc.vector.tensor_copy(u[1][:].rearrange("p (c i) h -> p c h i", i=2), pairs[1][:].rearrange("p h (c i) -> p c h i", i=2))
+        u_mx = [quantize("u%d" % g, u[g][:].rearrange("p s h -> p (s h)").bitcast(BF16)) for g in range(2)]
 
         scores = [ps.tile([P, N], F32, name="scores%d" % b, tag="wide", bufs=2) for b in range(QB)]
         for g in range(2):
@@ -129,7 +129,7 @@ def tile_attend_at_rope_f_topk_kernel(tc, qT, kT, cT, wT, vT, ls, us, offs, offs
                 nc.tensor.matmul_mx(scores[b][:, g * HALF : (g + 1) * HALF], q_codes[:, cols].bitcast(FP8X4), q_scales[:, cols],
                                     u_mx[g][0][:].bitcast(FP8X4), u_mx[g][1][:], start=True, stop=True)
 
-        y = sb.tile([P, QB, P, PACK], BF16, name="y", tag="value1", align_bytes=64)
+        y = sb.tile([P, QB, P, PACK], BF16, name="y", tag="value2", align_bytes=64)
         turned = []
         for b in range(QB):
             e = sb.tile([P, PACK, P], F32, name="e%d" % b)
@@ -139,44 +139,45 @@ def tile_attend_at_rope_f_topk_kernel(tc, qT, kT, cT, wT, vT, ls, us, offs, offs
                 nc.tensor.transpose(e_t[:, r, :], e[:, r, :], ident[:])
             turned.append(e_t)
 
-        def turn_values(j, tag, grouped):
-            vg = sb.tile([P, N], BF16, name="vg%d" % j, tag=tag, align_bytes=64)
+        def turn_values(j, grouped):
+            vg = sb.tile([P, N], BF16, name="vg%d" % j, align_bytes=64)
             nc.vector.tensor_copy(vg[:], values[j][:].indirect(tok_list[:]))
             words = vg[:].bitcast(F32)
-            v_t = ps.tile([P, 2, P], F32, name="v_t", bufs=2)
+            v_t = ps.tile([P, 2, P], F32, name="v_t", bufs=4)
             for h in range(2):
                 nc.tensor.transpose(v_t[:, h, :], words[:, h : N // 2 : 2], ident[:])
             nc.scalar.copy(grouped.rearrange("p (e h) -> p e h", h=2), v_t[:].rearrange("p h e -> p e h"))
 
         out_rows = out[0].rearrange("(p b) e -> p b e", b=QB)
 
-        def multiply(j, codes, scales):
-            acc = ps.tile([P, QB, P], F32, name="acc", bufs=2)
-            for b in range(QB):
+        def multiply(first, width, codes, scales, tag, bufs):
+            result = sb.tile([P, QB, width], F32, name="result%d" % first)
+            for b, copy in enumerate((nc.vector.tensor_copy, nc.scalar.copy)):
                 cols = slice(b * P, (b + 1) * P)
-                nc.tensor.matmul_mx(acc[:, b, :], y_codes[:, cols].bitcast(FP8X4), y_scales[:, cols],
-                                    codes.bitcast(FP8X4), scales, start=True, stop=True)
-            result = sb.tile([P, QB, P], F32, name="result%d" % j)
-            nc.scalar.copy(result[:], acc[:])
-            nc.sync.dma_start(out=out_rows[:, :, j * P : (j + 1) * P], in_=result[:])
+                acc = ps.tile([P, width], F32, name="acc", tag=tag, bufs=bufs)
+                nc.tensor.matmul_mx(acc[:], y_codes[:, cols].bitcast(FP8X4), y_scales[:, cols],
+                                    codes[:].bitcast(FP8X4), scales[:], start=True, stop=True)
+                copy(result[:, b, :], acc[:])
+            nc.sync.dma_start(out=out_rows[:, :, first : first + width], in_=result[:])
 
         v01 = sb.tile([P, 2 * 2 * P], F32, name="v01", align_bytes=64)
-        turn_values(0, "u1", v01[:, 0 : 2 * P])
-        turn_values(1, "", v01[:, 2 * P : 4 * P])
-
-        for b in range(QB):
-            nc.vector.tensor_tensor(y[:, b], turned[b][:].rearrange("p r q -> p q r"),
-                                    slot_scale[:].unsqueeze(1).broadcast_to([P, P, PACK]), ALU.mult)
-        v_codes, v_scales = quantize("v01", v01[:].bitcast(BF16))
-        y_codes, y_scales = quantize("y", y[:].rearrange("p b q r -> p (b q r)"))
-        for j in range(2):
-            multiply(j, v_codes[:, j * P : (j + 1) * P], v_scales[:, j * P : (j + 1) * P])
-
         v2 = sb.tile([P, 2 * P], F32, name="v2", align_bytes=64)
         v3 = sb.tile([P, 2 * P], F32, name="v3", align_bytes=64)
-        turn_values(2, "value1", v2[:])
-        turn_values(3, "", v3[:])
-        v_codes, v_scales = quantize("v2", v2[:].bitcast(BF16), tag="value3")
-        multiply(2, v_codes[:], v_scales[:])
+        turn_values(0, v01[:, 0 : 2 * P])
+        turn_values(1, v01[:, 2 * P : 4 * P])
+        turn_values(2, v2[:])
+        planes = sb.tile([P, PACK, P], BF16, name="planes")
+        for r in range(PACK):
+            nc.scalar.activation(planes[:, r, :], turned[0][:, r, :], ACT.Copy, scale=slot_scale[:, r : r + 1])
+        nc.scalar.copy(y[:, 0].rearrange("p (c i) r -> p c r i", i=4), planes[:].rearrange("p r (c i) -> p c r i", i=4))
+        nc.vector.tensor_tensor(y[:, 1], turned[1][:].rearrange("p r q -> p q r"),
+                                slot_scale[:].unsqueeze(1).broadcast_to([P, P, PACK]), ALU.mult)
+        turn_values(3, v3[:])
+        late = sb.tile([P, 5 * P], U32, name="late", tag="value3", align_bytes=64)
+        y_codes, y_scales = quantize("y", y[:].rearrange("p b q r -> p (b q r)"), late[:, 0 : 2 * P])
+        v01_mx = quantize("v01", v01[:].bitcast(BF16), late[:, 2 * P : 4 * P])
+        v2_mx = quantize("v2", v2[:].bitcast(BF16), late[:, 4 * P : 5 * P])
         v_codes, v_scales = quantize("v3", v3[:].bitcast(BF16))
-        multiply(3, v_codes[:], v_scales[:])
+        multiply(0, 2 * P, *v01_mx, "wide", 2)
+        multiply(2 * P, P, *v2_mx, "turned", 2)
+        multiply(3 * P, P, v_codes, v_scales, "v_t", 4)

@@ -29,9 +29,9 @@ def tile_attend_at_rope_f_topk_kernel(tc, qT, kT, cT, wT, vT, ls, us, offs, offs
         sb = ctx.enter_context(tc.tile_pool(name="sb", bufs=1))
         ps = ctx.enter_context(tc.psum_pool(name="ps", bufs=1))
 
-        def load(name, shape, dtype, src, tag=""):
+        def load(name, shape, dtype, src, tag="", queue=nc.sync):
             tile = sb.tile(shape, dtype, name=name, tag=tag, align_bytes=64)
-            nc.sync.dma_start(out=tile[:], in_=src)
+            queue.dma_start(out=tile[:], in_=src)
             return tile
 
         def quantize(name, source, codes=None):
@@ -54,8 +54,8 @@ def tile_attend_at_rope_f_topk_kernel(tc, qT, kT, cT, wT, vT, ls, us, offs, offs
         tok_list = load("tok_list", [P, N // 16], U16, offs)
         keys = [load("key%d" % t, [P, T], F32, k_rows[:, t, :]) for t in range(PACK)]
         q_raw = load("q_raw", [P, PACK, NQ], F32, qT[0].rearrange("(p t) q -> p t q", t=PACK))
-        lse = load("lse", [P, QB], F32, ls[0, 0].rearrange("(p b) -> p b", b=QB))
-        slot_scale = load("slot_scale", [P, PACK], F32, us[0].rearrange("(s r) o -> s (r o)", r=PACK))
+        lse = load("lse", [P, QB], F32, ls[0, 0].rearrange("(p b) -> p b", b=QB), queue=nc.gpsimd)
+        slot_scale = load("slot_scale", [P, PACK], F32, us[0].rearrange("(s r) o -> s (r o)", r=PACK), queue=nc.gpsimd)
         values = [load("value%d" % j, [P, T], F32, vT[j * P : (j + 1) * P, :], tag="value%d" % j) for j in range(VB)]
 
         ident = sb.tile([P, P], F32, name="ident")
@@ -72,15 +72,24 @@ def tile_attend_at_rope_f_topk_kernel(tc, qT, kT, cT, wT, vT, ls, us, offs, offs
             nc.scalar.mul(tile[:, 0, :], tile[:, 2, :], -1.0)
             trig.append(tile)
 
+        woven = sb.tile([P, 2, N, 2], F32, name="woven")
+        for odd in range(2):
+            nc.scalar.copy(woven[:, odd], trig[1][:, 1 - odd : 3 - odd, :].rearrange("p t s -> p s t"))
+
         def products(t):
             h, odd = divmod(t, 2)
             picked = [sb.tile([P, HALF], F32, name="picked%d_%d" % (t, g)) for g in range(2)]
-            terms = [sb.tile([P, 2, HALF], F32, name="terms%d_%d" % (t, g)) for g in range(2)]
+            terms = [sb.tile([P, 2 * HALF], F32, name="terms%d_%d" % (t, g)) for g in range(2)]
             for g in range(2):
                 nc.vector.tensor_copy(picked[g][:], keys[t][:].indirect(tok_list[:, g * HALF // 16 : (g + 1) * HALF // 16]))
             for g in range(2):
-                factors = trig[h][:, 1 - odd : 3 - odd, g * HALF : (g + 1) * HALF]
-                nc.vector.tensor_tensor(terms[g][:], factors, picked[g][:].unsqueeze(1).broadcast_to([P, 2, HALF]), ALU.mult)
+                slots = slice(g * HALF, (g + 1) * HALF)
+                if h == 0:
+                    nc.vector.tensor_tensor(terms[g][:].rearrange("p (t s) -> p t s", t=2), trig[0][:, 1 - odd : 3 - odd, slots],
+                                            picked[g][:].unsqueeze(1).broadcast_to([P, 2, HALF]), ALU.mult)
+                else:
+                    nc.vector.tensor_tensor(terms[g][:].rearrange("p (s t) -> p s t", t=2), woven[:, odd, slots, :],
+                                            picked[g][:].unsqueeze(2).broadcast_to([P, HALF, 2]), ALU.mult)
             return terms
 
         pairs = [sb.tile([P, 2, HALF], F32, name="pairs%d" % g) for g in range(2)]
@@ -91,9 +100,9 @@ def tile_attend_at_rope_f_topk_kernel(tc, qT, kT, cT, wT, vT, ls, us, offs, offs
             sums = ps.tile([P, 2, 2, P], F32, name="sums", tag="wide", bufs=2)
             for c in range(2):
                 for t in range(2):
-                    cols = slice(c * P, (c + 1) * P)
-                    nc.tensor.matmul(sums[:, c, t, :], even[g][:, t, cols], ident[:], start=True, stop=False, is_transpose=True)
-                    nc.tensor.matmul(sums[:, c, t, :], odd[g][:, t, cols], ident[:], start=False, stop=True, is_transpose=True)
+                    cols = slice(t * HALF + c * P, t * HALF + (c + 1) * P)
+                    nc.tensor.matmul(sums[:, c, t, :], even[g][:, cols], ident[:], start=True, stop=False, is_transpose=True)
+                    nc.tensor.matmul(sums[:, c, t, :], odd[g][:, cols], ident[:], start=False, stop=True, is_transpose=True)
             rounded = sb.tile([P, 2, P, 2], BF16, name="rounded%d" % g)
             nc.scalar.copy(rounded[:], sums[:].rearrange("s c t p -> s c p t"))
             rounded_words = rounded[:].rearrange("s c p t -> s (c p t)").bitcast(F32)
@@ -104,12 +113,7 @@ def tile_attend_at_rope_f_topk_kernel(tc, qT, kT, cT, wT, vT, ls, us, offs, offs
 
         even, odd = products(2), products(3)
         for g in range(2):
-            nc.vector.tensor_tensor(
-                pairs[g][:, 1, :].bitcast(BF16).rearrange("p (c i t) -> p c t i", i=4, t=2),
-                even[g][:].rearrange("p t (c i) -> p c t i", i=4),
-                odd[g][:].rearrange("p t (c i) -> p c t i", i=4),
-                ALU.add,
-            )
+            nc.vector.tensor_tensor(pairs[g][:, 1, :].bitcast(BF16), even[g][:], odd[g][:], ALU.add)
 
         q_grouped = sb.tile([P, QB, P, PACK], BF16, name="q_grouped", align_bytes=64)
         nc.scalar.copy(q_grouped[:], q_raw[:].rearrange("p t (m b) -> p b m t", b=QB))
@@ -119,24 +123,32 @@ def tile_attend_at_rope_f_topk_kernel(tc, qT, kT, cT, wT, vT, ls, us, offs, offs
 
         u = [sb.tile([P, HALF, 2], F32, name="u%d" % g, align_bytes=64) for g in range(2)]
         nc.scalar.copy(u[0][:], pairs[0][:].rearrange("p h s -> p s h"))
-        nc.vector.tensor_copy(u[1][:].rearrange("p (c i) h -> p c h i", i=2), pairs[1][:].rearrange("p h (c i) -> p c h i", i=2))
+        nc.vector.tensor_copy(u[1][:], pairs[1][:].rearrange("p h s -> p s h"))
         u_mx = [quantize("u%d" % g, u[g][:].rearrange("p s h -> p (s h)").bitcast(BF16)) for g in range(2)]
 
-        scores = [ps.tile([P, N], F32, name="scores%d" % b, tag="wide", bufs=2) for b in range(QB)]
+        first_half = ps.tile([P, QB, HALF], F32, name="first_half", tag="wide", bufs=2)
+        scores = [
+            [first_half[:, 0, :], first_half[:, 1, :]],
+            [ps.tile([P, HALF], F32, name="second_half0", tag="wide", bufs=2)[:],
+             ps.tile([P, HALF], F32, name="second_half1", tag="v_t", bufs=4)[:]],
+        ]
+        e = [sb.tile([P, PACK, P], F32, name="e%d" % b) for b in range(QB)]
         for g in range(2):
             for b in range(QB):
                 cols = slice(b * P, (b + 1) * P)
-                nc.tensor.matmul_mx(scores[b][:, g * HALF : (g + 1) * HALF], q_codes[:, cols].bitcast(FP8X4), q_scales[:, cols],
+                nc.tensor.matmul_mx(scores[g][b], q_codes[:, cols].bitcast(FP8X4), q_scales[:, cols],
                                     u_mx[g][0][:].bitcast(FP8X4), u_mx[g][1][:], start=True, stop=True)
+            for b in range(QB):
+                nc.scalar.activation(e[b][:, :, g * P // 2 : (g + 1) * P // 2],
+                                     scores[g][b].rearrange("p (s r) -> p r s", r=PACK),
+                                     ACT.Exp, bias=neg_lse[:, b : b + 1])
 
         y = sb.tile([P, QB, P, PACK], BF16, name="y", tag="value2", align_bytes=64)
         turned = []
         for b in range(QB):
-            e = sb.tile([P, PACK, P], F32, name="e%d" % b)
-            nc.scalar.activation(e[:], scores[b][:].rearrange("p (s r) -> p r s", r=PACK), ACT.Exp, bias=neg_lse[:, b : b + 1])
             e_t = ps.tile([P, PACK, P], F32, name="e_t%d" % b, tag="turned", bufs=2)
             for r in range(PACK):
-                nc.tensor.transpose(e_t[:, r, :], e[:, r, :], ident[:])
+                nc.tensor.transpose(e_t[:, r, :], e[b][:, r, :], ident[:])
             turned.append(e_t)
 
         def turn_values(j, grouped):
@@ -168,9 +180,9 @@ def tile_attend_at_rope_f_topk_kernel(tc, qT, kT, cT, wT, vT, ls, us, offs, offs
         turn_values(2, v2[:])
         planes = sb.tile([P, PACK, P], BF16, name="planes")
         for r in range(PACK):
-            nc.scalar.activation(planes[:, r, :], turned[0][:, r, :], ACT.Copy, scale=slot_scale[:, r : r + 1])
-        nc.scalar.copy(y[:, 0].rearrange("p (c i) r -> p c r i", i=4), planes[:].rearrange("p r (c i) -> p c r i", i=4))
-        nc.vector.tensor_tensor(y[:, 1], turned[1][:].rearrange("p r q -> p q r"),
+            nc.scalar.activation(planes[:, r, :], turned[1][:, r, :], ACT.Copy, scale=slot_scale[:, r : r + 1])
+        nc.scalar.copy(y[:, 1].rearrange("p (c i) r -> p c r i", i=4), planes[:].rearrange("p r (c i) -> p c r i", i=4))
+        nc.vector.tensor_tensor(y[:, 0], turned[0][:].rearrange("p r q -> p q r"),
                                 slot_scale[:].unsqueeze(1).broadcast_to([P, P, PACK]), ALU.mult)
         turn_values(3, v3[:])
         late = sb.tile([P, 5 * P], U32, name="late", tag="value3", align_bytes=64)

@@ -46,11 +46,11 @@ def tile_attend_at_rope_f_topk_kernel(tc, qT, kT, cT, wT, vT, ls, us, offs, offs
         c_rows = cT.rearrange("(p t) n -> p t n", t=PACK)
         w_rows = wT.rearrange("(p t) n -> p t n", t=PACK)
 
+        cos = [load("cos0", [P, TP], F32, c_rows[:, 0, :])]
         pos_list = load("pos_list", [P, N // 16], U16, offs2)
-        cos, sin = [], []
-        for h in range(2):
-            cos.append(load("cos%d" % h, [P, TP], F32, c_rows[:, 2 * h, :]))
-            sin.append(load("sin%d" % h, [P, TP], F32, w_rows[:, 2 * h, :]))
+        sin = [load("sin0", [P, TP], F32, w_rows[:, 0, :])]
+        cos.append(load("cos1", [P, TP], F32, c_rows[:, 2, :]))
+        sin.append(load("sin1", [P, TP], F32, w_rows[:, 2, :]))
         tok_list = load("tok_list", [P, N // 16], U16, offs)
         keys = [load("key%d" % t, [P, T], F32, k_rows[:, t, :]) for t in range(PACK)]
         q_raw = load("q_raw", [P, PACK, NQ], F32, qT[0].rearrange("(p t) q -> p t q", t=PACK))
@@ -143,13 +143,19 @@ def tile_attend_at_rope_f_topk_kernel(tc, qT, kT, cT, wT, vT, ls, us, offs, offs
                                      scores[g][b].rearrange("p (s r) -> p r s", r=PACK),
                                      ACT.Exp, bias=neg_lse[:, b : b + 1])
 
-        y = sb.tile([P, QB, P, PACK], BF16, name="y", tag="value2", align_bytes=64)
+        y = sb.tile([P, QB, P, PACK], BF16, name="y", align_bytes=64)
         turned = []
         for b in range(QB):
             e_t = ps.tile([P, PACK, P], F32, name="e_t%d" % b, tag="turned", bufs=2)
             for r in range(PACK):
                 nc.tensor.transpose(e_t[:, r, :], e[b][:, r, :], ident[:])
             turned.append(e_t)
+
+        for b in range(QB):
+            planes = sb.tile([P, PACK, P], BF16, name="planes%d" % b)
+            for r in range(PACK):
+                nc.scalar.activation(planes[:, r, :], turned[b][:, r, :], ACT.Copy, scale=slot_scale[:, r : r + 1])
+            nc.scalar.copy(y[:, b].rearrange("p (c i) r -> p c r i", i=4), planes[:].rearrange("p r (c i) -> p c r i", i=4))
 
         def turn_values(j, grouped):
             vg = sb.tile([P, N], BF16, name="vg%d" % j, align_bytes=64)
@@ -178,12 +184,6 @@ def tile_attend_at_rope_f_topk_kernel(tc, qT, kT, cT, wT, vT, ls, us, offs, offs
         turn_values(0, v01[:, 0 : 2 * P])
         turn_values(1, v01[:, 2 * P : 4 * P])
         turn_values(2, v2[:])
-        planes = sb.tile([P, PACK, P], BF16, name="planes")
-        for r in range(PACK):
-            nc.scalar.activation(planes[:, r, :], turned[1][:, r, :], ACT.Copy, scale=slot_scale[:, r : r + 1])
-        nc.scalar.copy(y[:, 1].rearrange("p (c i) r -> p c r i", i=4), planes[:].rearrange("p r (c i) -> p c r i", i=4))
-        nc.vector.tensor_tensor(y[:, 0], turned[0][:].rearrange("p r q -> p q r"),
-                                slot_scale[:].unsqueeze(1).broadcast_to([P, P, PACK]), ALU.mult)
         turn_values(3, v3[:])
         late = sb.tile([P, 5 * P], U32, name="late", tag="value3", align_bytes=64)
         y_codes, y_scales = quantize("y", y[:].rearrange("p b q r -> p (b q r)"), late[:, 0 : 2 * P])

@@ -21,6 +21,11 @@ PACK = 4
 QB = NQ // P
 VB = DV // P
 HALF = N // 2
+LIST_HALF = HALF // 16
+
+SUMS = dict(tag="sums", bufs=2)
+TURNS = dict(tag="turns", bufs=2)
+VALUE_TURNS = dict(tag="value_turns", bufs=4)
 
 
 def tile_attend_at_rope_f_topk_kernel(tc, qT, kT, cT, wT, vT, ls, us, offs, offs2, out):
@@ -29,91 +34,96 @@ def tile_attend_at_rope_f_topk_kernel(tc, qT, kT, cT, wT, vT, ls, us, offs, offs
         sb = ctx.enter_context(tc.tile_pool(name="sb", bufs=1))
         ps = ctx.enter_context(tc.psum_pool(name="ps", bufs=1))
 
-        def load(name, shape, dtype, src, tag="", queue=nc.sync):
-            tile = sb.tile(shape, dtype, name=name, tag=tag, align_bytes=64)
-            queue.dma_start(out=tile[:], in_=src)
+        def load(name, shape, dtype, src):
+            tile = sb.tile(shape, dtype, name=name, tag=name, align_bytes=64)
+            nc.sync.dma_start(out=tile[:], in_=src)
             return tile
 
-        def quantize(name, source, codes=None):
-            words = source.shape[1] // PACK
-            if codes is None:
-                codes = sb.tile([P, words], U32, name=name + "_codes", align_bytes=64)
-            scales = sb.tile([P, words], U8, name=name + "_scales", align_bytes=64)
-            nc.vector.quantize_mx(codes[:].bitcast(FP8X4), scales[:], source)
-            return codes, scales
+        def quantize_into(codes, name, source):
+            scales = sb.tile([P, codes.shape[1]], U8, name=name + "_scales", align_bytes=64)
+            nc.vector.quantize_mx(codes.bitcast(FP8X4), scales[:], source)
+            return codes, scales[:]
 
-        k_rows = kT.rearrange("(p t) n -> p t n", t=PACK)
-        c_rows = cT.rearrange("(p t) n -> p t n", t=PACK)
-        w_rows = wT.rearrange("(p t) n -> p t n", t=PACK)
+        def quantize(name, source):
+            codes = sb.tile([P, source.shape[1] // PACK], U32, name=name + "_codes", align_bytes=64)
+            return quantize_into(codes[:], name, source)
 
-        cos = [load("cos0", [P, TP], F32, c_rows[:, 0, :])]
+        def by_place(table):
+            return table.rearrange("(p t) n -> p t n", t=PACK)
+
+        cos = load("cos", [P, 2, TP], F32, by_place(cT)[:, 1:3, :])
         pos_list = load("pos_list", [P, N // 16], U16, offs2)
-        sin = [load("sin0", [P, TP], F32, w_rows[:, 0, :])]
-        cos.append(load("cos1", [P, TP], F32, c_rows[:, 2, :]))
-        sin.append(load("sin1", [P, TP], F32, w_rows[:, 2, :]))
+        sin = load("sin", [P, 2, TP], F32, by_place(wT)[:, 1:3, :])
         tok_list = load("tok_list", [P, N // 16], U16, offs)
-        keys = [load("key%d" % t, [P, T], F32, k_rows[:, t, :]) for t in range(PACK)]
-        q_raw = load("q_raw", [P, PACK, NQ], F32, qT[0].rearrange("(p t) q -> p t q", t=PACK))
-        lse = load("lse", [P, QB], F32, ls[0, 0].rearrange("(p b) -> p b", b=QB), queue=nc.gpsimd)
-        slot_scale = load("slot_scale", [P, PACK], F32, us[0].rearrange("(s r) o -> s (r o)", r=PACK), queue=nc.gpsimd)
-        values = [load("value%d" % j, [P, T], F32, vT[j * P : (j + 1) * P, :], tag="value%d" % j) for j in range(VB)]
+        keys = [load("key%d" % t, [P, T], F32, by_place(kT)[:, t, :]) for t in range(PACK)]
+        q_raw = load("q_raw", [P, PACK, NQ], F32, by_place(qT[0]))
+        lse = load("lse", [P, QB], F32, ls[0, 0].rearrange("(m b) -> m b", b=QB))
+        slot_scale = load("slot_scale", [P, PACK], F32, us[0].rearrange("(s r) o -> s (r o)", r=PACK))
+        values = [load("value%d" % j, [P, T], F32, vT[j * P : (j + 1) * P, :]) for j in range(VB)]
 
         ident = sb.tile([P, P], F32, name="ident")
         make_identity(nc, ident[:])
 
-        warm = sb.tile([P, 1], F32, name="warm")
-        nc.scalar.activation(warm[:], ident[:, 0:1], ACT.Exp)
-
-        trig = []
+        trig = [sb.tile([P, 3, N], F32, name="trig%d" % h) for h in range(2)]
         for h in range(2):
-            tile = sb.tile([P, 3, N], F32, name="trig%d" % h)
-            nc.vector.tensor_copy(tile[:, 1, :], cos[h][:].indirect(pos_list[:]))
-            nc.vector.tensor_copy(tile[:, 2, :], sin[h][:].indirect(pos_list[:]))
-            nc.scalar.mul(tile[:, 0, :], tile[:, 2, :], -1.0)
-            trig.append(tile)
+            nc.vector.tensor_copy(trig[h][:, 1, :], cos[:, h, :].indirect(pos_list[:]))
+        for h in range(2):
+            nc.vector.tensor_copy(trig[h][:, 2, :], sin[:, h, :].indirect(pos_list[:]))
+            nc.scalar.mul(trig[h][:, 0, :], trig[h][:, 2, :], -1.0)
+
+        def factors(h, odd):
+            return trig[h][:, 1 - odd : 3 - odd, :]
 
         woven = sb.tile([P, 2, N, 2], F32, name="woven")
         for odd in range(2):
-            nc.scalar.copy(woven[:, odd], trig[1][:, 1 - odd : 3 - odd, :].rearrange("p t s -> p s t"))
+            nc.scalar.copy(woven[:, odd], factors(1, odd).rearrange("p t s -> p s t"))
 
-        def products(t):
-            h, odd = divmod(t, 2)
+        def gather_keys(t):
             picked = [sb.tile([P, HALF], F32, name="picked%d_%d" % (t, g)) for g in range(2)]
-            terms = [sb.tile([P, 2 * HALF], F32, name="terms%d_%d" % (t, g)) for g in range(2)]
             for g in range(2):
-                nc.vector.tensor_copy(picked[g][:], keys[t][:].indirect(tok_list[:, g * HALF // 16 : (g + 1) * HALF // 16]))
+                nc.vector.tensor_copy(picked[g][:], keys[t][:].indirect(tok_list[:, g * LIST_HALF : (g + 1) * LIST_HALF]))
+            return picked
+
+        def first_pair_terms(odd):
+            picked = gather_keys(odd)
+            terms = [sb.tile([P, 2, HALF], F32, name="terms%d_%d" % (odd, g)) for g in range(2)]
             for g in range(2):
-                slots = slice(g * HALF, (g + 1) * HALF)
-                if h == 0:
-                    nc.vector.tensor_tensor(terms[g][:].rearrange("p (t s) -> p t s", t=2), trig[0][:, 1 - odd : 3 - odd, slots],
-                                            picked[g][:].unsqueeze(1).broadcast_to([P, 2, HALF]), ALU.mult)
-                else:
-                    nc.vector.tensor_tensor(terms[g][:].rearrange("p (s t) -> p s t", t=2), woven[:, odd, slots, :],
-                                            picked[g][:].unsqueeze(2).broadcast_to([P, HALF, 2]), ALU.mult)
+                nc.vector.tensor_tensor(terms[g][:], factors(0, odd)[:, :, g * HALF : (g + 1) * HALF],
+                                        picked[g][:].unsqueeze(1).broadcast_to([P, 2, HALF]), ALU.mult)
+            return terms
+
+        def second_pair_terms(odd):
+            picked = gather_keys(2 + odd)
+            terms = [sb.tile([P, HALF, 2], F32, name="terms%d_%d" % (2 + odd, g)) for g in range(2)]
+            for g in range(2):
+                nc.vector.tensor_tensor(terms[g][:], woven[:, odd, g * HALF : (g + 1) * HALF, :],
+                                        picked[g][:].unsqueeze(2).broadcast_to([P, HALF, 2]), ALU.mult)
             return terms
 
         pairs = [sb.tile([P, 2, HALF], F32, name="pairs%d" % g) for g in range(2)]
 
-        even, odd = products(0), products(1)
-        back = ps.tile([P, 2, HALF], F32, name="back", tag="turned", bufs=2)
+        even_terms, odd_terms = first_pair_terms(0), first_pair_terms(1)
+        turned_back = ps.tile([P, 2, HALF], F32, name="turned_back", **TURNS)
         for g in range(2):
-            sums = ps.tile([P, 2, 2, P], F32, name="sums", tag="wide", bufs=2)
+            sums = ps.tile([P, 2, 2, P], F32, name="sums", **SUMS)
             for c in range(2):
+                chunk = slice(c * P, (c + 1) * P)
                 for t in range(2):
-                    cols = slice(t * HALF + c * P, t * HALF + (c + 1) * P)
-                    nc.tensor.matmul(sums[:, c, t, :], even[g][:, cols], ident[:], start=True, stop=False, is_transpose=True)
-                    nc.tensor.matmul(sums[:, c, t, :], odd[g][:, cols], ident[:], start=False, stop=True, is_transpose=True)
+                    nc.tensor.matmul(sums[:, c, t, :], even_terms[g][:, t, chunk], ident[:], start=True, stop=False, is_transpose=True)
+                    nc.tensor.matmul(sums[:, c, t, :], odd_terms[g][:, t, chunk], ident[:], start=False, stop=True, is_transpose=True)
             rounded = sb.tile([P, 2, P, 2], BF16, name="rounded%d" % g)
             nc.scalar.copy(rounded[:], sums[:].rearrange("s c t p -> s c p t"))
             rounded_words = rounded[:].rearrange("s c p t -> s (c p t)").bitcast(F32)
             for c in range(2):
-                nc.tensor.transpose(back[:, g, c * P : (c + 1) * P], rounded_words[:, c * P : (c + 1) * P], ident[:])
+                chunk = slice(c * P, (c + 1) * P)
+                nc.tensor.transpose(turned_back[:, g, chunk], rounded_words[:, chunk], ident[:])
         for g in range(2):
-            nc.scalar.copy(pairs[g][:, 0, :], back[:, g, :])
+            nc.scalar.copy(pairs[g][:, 0, :], turned_back[:, g, :])
 
-        even, odd = products(2), products(3)
+        even_terms, odd_terms = second_pair_terms(0), second_pair_terms(1)
         for g in range(2):
-            nc.vector.tensor_tensor(pairs[g][:, 1, :].bitcast(BF16), even[g][:], odd[g][:], ALU.add)
+            nc.vector.tensor_tensor(pairs[g][:, 1, :].bitcast(BF16), even_terms[g][:].rearrange("p s t -> p (s t)"),
+                                    odd_terms[g][:].rearrange("p s t -> p (s t)"), ALU.add)
 
         q_grouped = sb.tile([P, QB, P, PACK], BF16, name="q_grouped", align_bytes=64)
         nc.scalar.copy(q_grouped[:], q_raw[:].rearrange("p t (m b) -> p b m t", b=QB))
@@ -122,74 +132,77 @@ def tile_attend_at_rope_f_topk_kernel(tc, qT, kT, cT, wT, vT, ls, us, offs, offs
         q_codes, q_scales = quantize("q", q_grouped[:].rearrange("p b m t -> p (b m t)"))
 
         u = [sb.tile([P, HALF, 2], F32, name="u%d" % g, align_bytes=64) for g in range(2)]
-        nc.scalar.copy(u[0][:], pairs[0][:].rearrange("p h s -> p s h"))
-        nc.vector.tensor_copy(u[1][:], pairs[1][:].rearrange("p h s -> p s h"))
+        for g, copy in enumerate((nc.scalar.copy, nc.vector.tensor_copy)):
+            copy(u[g][:], pairs[g][:].rearrange("p h s -> p s h"))
         u_mx = [quantize("u%d" % g, u[g][:].rearrange("p s h -> p (s h)").bitcast(BF16)) for g in range(2)]
 
-        first_half = ps.tile([P, QB, HALF], F32, name="first_half", tag="wide", bufs=2)
-        scores = [
-            [first_half[:, 0, :], first_half[:, 1, :]],
-            [ps.tile([P, HALF], F32, name="second_half0", tag="wide", bufs=2)[:],
-             ps.tile([P, HALF], F32, name="second_half1", tag="v_t", bufs=4)[:]],
-        ]
+        first_half = ps.tile([P, QB, HALF], F32, name="first_half", **SUMS)
+        second_half = [ps.tile([P, HALF], F32, name="second_half%d" % b, **ring) for b, ring in enumerate((SUMS, VALUE_TURNS))]
+        scores = [[first_half[:, b, :] for b in range(QB)], [second_half[b][:] for b in range(QB)]]
         e = [sb.tile([P, PACK, P], F32, name="e%d" % b) for b in range(QB)]
         for g in range(2):
+            u_codes, u_scales = u_mx[g]
             for b in range(QB):
                 cols = slice(b * P, (b + 1) * P)
                 nc.tensor.matmul_mx(scores[g][b], q_codes[:, cols].bitcast(FP8X4), q_scales[:, cols],
-                                    u_mx[g][0][:].bitcast(FP8X4), u_mx[g][1][:], start=True, stop=True)
+                                    u_codes.bitcast(FP8X4), u_scales, start=True, stop=True)
             for b in range(QB):
-                nc.scalar.activation(e[b][:, :, g * P // 2 : (g + 1) * P // 2],
+                nc.scalar.activation(e[b][:, :, g * HALF // PACK : (g + 1) * HALF // PACK],
                                      scores[g][b].rearrange("p (s r) -> p r s", r=PACK),
                                      ACT.Exp, bias=neg_lse[:, b : b + 1])
 
         y = sb.tile([P, QB, P, PACK], BF16, name="y", align_bytes=64)
-        turned = []
+        e_turned = []
         for b in range(QB):
-            e_t = ps.tile([P, PACK, P], F32, name="e_t%d" % b, tag="turned", bufs=2)
+            bank = ps.tile([P, PACK, P], F32, name="e_turned%d" % b, **TURNS)
             for r in range(PACK):
-                nc.tensor.transpose(e_t[:, r, :], e[b][:, r, :], ident[:])
-            turned.append(e_t)
+                nc.tensor.transpose(bank[:, r, :], e[b][:, r, :], ident[:])
+            e_turned.append(bank)
 
         for b in range(QB):
-            planes = sb.tile([P, PACK, P], BF16, name="planes%d" % b)
+            y_rows = sb.tile([P, PACK, P], BF16, name="y_rows%d" % b)
             for r in range(PACK):
-                nc.scalar.activation(planes[:, r, :], turned[b][:, r, :], ACT.Copy, scale=slot_scale[:, r : r + 1])
-            nc.scalar.copy(y[:, b].rearrange("p (c i) r -> p c r i", i=4), planes[:].rearrange("p r (c i) -> p c r i", i=4))
+                nc.scalar.activation(y_rows[:, r, :], e_turned[b][:, r, :], ACT.Copy, scale=slot_scale[:, r : r + 1])
+            nc.scalar.copy(y[:, b].rearrange("p (c i) r -> p c r i", i=4), y_rows[:].rearrange("p r (c i) -> p c r i", i=4))
 
         def turn_values(j, grouped):
-            vg = sb.tile([P, N], BF16, name="vg%d" % j, align_bytes=64)
-            nc.vector.tensor_copy(vg[:], values[j][:].indirect(tok_list[:]))
-            words = vg[:].bitcast(F32)
-            v_t = ps.tile([P, 2, P], F32, name="v_t", bufs=4)
+            gathered = sb.tile([P, N], BF16, name="gathered%d" % j, align_bytes=64)
+            nc.vector.tensor_copy(gathered[:], values[j][:].indirect(tok_list[:]))
+            words = gathered[:].bitcast(F32)
+            bank = ps.tile([P, 2, P], F32, name="v_turned", **VALUE_TURNS)
             for h in range(2):
-                nc.tensor.transpose(v_t[:, h, :], words[:, h : N // 2 : 2], ident[:])
-            nc.scalar.copy(grouped.rearrange("p (e h) -> p e h", h=2), v_t[:].rearrange("p h e -> p e h"))
+                nc.tensor.transpose(bank[:, h, :], words[:, h : N // 2 : 2], ident[:])
+            nc.scalar.copy(grouped.rearrange("p (e h) -> p e h", h=2), bank[:].rearrange("p h e -> p e h"))
 
-        out_rows = out[0].rearrange("(p b) e -> p b e", b=QB)
+        out_rows = out[0].rearrange("(m b) e -> m b e", b=QB)
+        results = [sb.tile([P, QB, DV // 2], F32, name="result%d" % i) for i in range(2)]
 
-        def multiply(first, width, codes, scales, tag, bufs):
-            result = sb.tile([P, QB, width], F32, name="result%d" % first)
+        def multiply(result, v_mx, ring):
+            v_codes, v_scales = v_mx
             for b, copy in enumerate((nc.vector.tensor_copy, nc.scalar.copy)):
                 cols = slice(b * P, (b + 1) * P)
-                acc = ps.tile([P, width], F32, name="acc", tag=tag, bufs=bufs)
+                acc = ps.tile([P, result.shape[2]], F32, name="acc", **ring)
                 nc.tensor.matmul_mx(acc[:], y_codes[:, cols].bitcast(FP8X4), y_scales[:, cols],
-                                    codes[:].bitcast(FP8X4), scales[:], start=True, stop=True)
+                                    v_codes.bitcast(FP8X4), v_scales, start=True, stop=True)
                 copy(result[:, b, :], acc[:])
-            nc.sync.dma_start(out=out_rows[:, :, first : first + width], in_=result[:])
 
-        v01 = sb.tile([P, 2 * 2 * P], F32, name="v01", align_bytes=64)
-        v2 = sb.tile([P, 2 * P], F32, name="v2", align_bytes=64)
-        v3 = sb.tile([P, 2 * P], F32, name="v3", align_bytes=64)
-        turn_values(0, v01[:, 0 : 2 * P])
-        turn_values(1, v01[:, 2 * P : 4 * P])
+        plane_words = 2 * P
+        v01 = sb.tile([P, 2 * plane_words], F32, name="v01", align_bytes=64)
+        v2 = sb.tile([P, plane_words], F32, name="v2", align_bytes=64)
+        v3 = sb.tile([P, plane_words], F32, name="v3", align_bytes=64)
+        turn_values(0, v01[:, 0:plane_words])
+        turn_values(1, v01[:, plane_words : 2 * plane_words])
         turn_values(2, v2[:])
         turn_values(3, v3[:])
-        late = sb.tile([P, 5 * P], U32, name="late", tag="value3", align_bytes=64)
-        y_codes, y_scales = quantize("y", y[:].rearrange("p b q r -> p (b q r)"), late[:, 0 : 2 * P])
-        v01_mx = quantize("v01", v01[:].bitcast(BF16), late[:, 2 * P : 4 * P])
-        v2_mx = quantize("v2", v2[:].bitcast(BF16), late[:, 4 * P : 5 * P])
-        v_codes, v_scales = quantize("v3", v3[:].bitcast(BF16))
-        multiply(0, 2 * P, *v01_mx, "wide", 2)
-        multiply(2 * P, P, *v2_mx, "turned", 2)
-        multiply(3 * P, P, v_codes, v_scales, "v_t", 4)
+
+        late_codes = sb.tile([P, NQ + 3 * P], U32, name="late_codes", tag="value3", align_bytes=64)
+        y_codes, y_scales = quantize_into(late_codes[:, 0:NQ], "y", y[:].rearrange("p b q r -> p (b q r)"))
+        v01_mx = quantize_into(late_codes[:, NQ : NQ + 2 * P], "v01", v01[:].bitcast(BF16))
+        v2_mx = quantize_into(late_codes[:, NQ + 2 * P : NQ + 3 * P], "v2", v2[:].bitcast(BF16))
+        v3_mx = quantize("v3", v3[:].bitcast(BF16))
+
+        multiply(results[0][:], v01_mx, SUMS)
+        nc.sync.dma_start(out=out_rows[:, :, 0 : DV // 2], in_=results[0][:])
+        multiply(results[1][:, :, 0:P], v2_mx, TURNS)
+        multiply(results[1][:, :, P : 2 * P], v3_mx, VALUE_TURNS)
+        nc.sync.dma_start(out=out_rows[:, :, DV // 2 : DV], in_=results[1][:])

from contextlib import ExitStack

import concourse.mybir as mybir
from concourse.masks import make_identity

D, NQ, T, TP, N, DV = 512, 256, 2048, 1024, 512, 512
FLOPS = 2 * D * N * NQ + 2 * N * NQ * DV
BYTES = 4 * (D * NQ + D * T + D * TP + DV * T + NQ + N + NQ * DV) + 2 * 2 * 128 * (N // 16)

F32 = mybir.dt.float32
BF16 = mybir.dt.bfloat16
U32 = mybir.dt.uint32
U16 = mybir.dt.uint16
U8 = mybir.dt.uint8
FP8X4 = mybir.dt.float8_e4m3fn_x4
ACT = mybir.ActivationFunctionType
ALU = mybir.AluOpType

P = 128
PACK = 4
QB = NQ // P
VB = DV // P
HALF = N // 2
LIST_HALF = HALF // 16

SUMS = dict(tag="sums", bufs=2)
TURNS = dict(tag="turns", bufs=2)
VALUE_TURNS = dict(tag="value_turns", bufs=4)


def tile_attend_at_rope_f_topk_kernel(tc, qT, kT, cT, wT, vT, ls, us, offs, offs2, out):
    nc = tc.nc
    with ExitStack() as ctx:
        sb = ctx.enter_context(tc.tile_pool(name="sb", bufs=1))
        ps = ctx.enter_context(tc.psum_pool(name="ps", bufs=1))

        def load(name, shape, dtype, src):
            tile = sb.tile(shape, dtype, name=name, tag=name, align_bytes=64)
            nc.sync.dma_start(out=tile[:], in_=src)
            return tile

        def quantize_into(codes, name, source):
            scales = sb.tile([P, codes.shape[1]], U8, name=name + "_scales", align_bytes=64)
            nc.vector.quantize_mx(codes.bitcast(FP8X4), scales[:], source)
            return codes, scales[:]

        def quantize(name, source):
            codes = sb.tile([P, source.shape[1] // PACK], U32, name=name + "_codes", align_bytes=64)
            return quantize_into(codes[:], name, source)

        def by_place(table):
            return table.rearrange("(p t) n -> p t n", t=PACK)

        cos = load("cos", [P, 2, TP], F32, by_place(cT)[:, 1:3, :])
        pos_list = load("pos_list", [P, N // 16], U16, offs2)
        sin = load("sin", [P, 2, TP], F32, by_place(wT)[:, 1:3, :])
        tok_list = load("tok_list", [P, N // 16], U16, offs)
        keys = [load("key%d" % t, [P, T], F32, by_place(kT)[:, t, :]) for t in range(PACK)]
        q_raw = load("q_raw", [P, PACK, NQ], F32, by_place(qT[0]))
        lse = load("lse", [P, QB], F32, ls[0, 0].rearrange("(m b) -> m b", b=QB))
        slot_scale = load("slot_scale", [P, PACK], F32, us[0].rearrange("(s r) o -> s (r o)", r=PACK))
        values = [load("value%d" % j, [P, T], F32, vT[j * P : (j + 1) * P, :]) for j in range(VB)]

        ident = sb.tile([P, P], F32, name="ident")
        make_identity(nc, ident[:])

        trig = [sb.tile([P, 3, N], F32, name="trig%d" % h) for h in range(2)]
        for h in range(2):
            nc.vector.tensor_copy(trig[h][:, 1, :], cos[:, h, :].indirect(pos_list[:]))
        for h in range(2):
            nc.vector.tensor_copy(trig[h][:, 2, :], sin[:, h, :].indirect(pos_list[:]))
            nc.scalar.mul(trig[h][:, 0, :], trig[h][:, 2, :], -1.0)

        def factors(h, odd):
            return trig[h][:, 1 - odd : 3 - odd, :]

        woven = sb.tile([P, 2, N, 2], F32, name="woven")
        for odd in range(2):
            nc.scalar.copy(woven[:, odd], factors(1, odd).rearrange("p t s -> p s t"))

        def gather_keys(t):
            picked = [sb.tile([P, HALF], F32, name="picked%d_%d" % (t, g)) for g in range(2)]
            for g in range(2):
                nc.vector.tensor_copy(picked[g][:], keys[t][:].indirect(tok_list[:, g * LIST_HALF : (g + 1) * LIST_HALF]))
            return picked

        def first_pair_terms(odd):
            picked = gather_keys(odd)
            terms = [sb.tile([P, 2, HALF], F32, name="terms%d_%d" % (odd, g)) for g in range(2)]
            for g in range(2):
                nc.vector.tensor_tensor(terms[g][:], factors(0, odd)[:, :, g * HALF : (g + 1) * HALF],
                                        picked[g][:].unsqueeze(1).broadcast_to([P, 2, HALF]), ALU.mult)
            return terms

        def second_pair_terms(odd):
            picked = gather_keys(2 + odd)
            terms = [sb.tile([P, HALF, 2], F32, name="terms%d_%d" % (2 + odd, g)) for g in range(2)]
            for g in range(2):
                nc.vector.tensor_tensor(terms[g][:], woven[:, odd, g * HALF : (g + 1) * HALF, :],
                                        picked[g][:].unsqueeze(2).broadcast_to([P, HALF, 2]), ALU.mult)
            return terms

        pairs = [sb.tile([P, 2, HALF], F32, name="pairs%d" % g) for g in range(2)]

        even_terms, odd_terms = first_pair_terms(0), first_pair_terms(1)
        turned_back = ps.tile([P, 2, HALF], F32, name="turned_back", **TURNS)
        for g in range(2):
            sums = ps.tile([P, 2, 2, P], F32, name="sums", **SUMS)
            for c in range(2):
                chunk = slice(c * P, (c + 1) * P)
                for t in range(2):
                    nc.tensor.matmul(sums[:, c, t, :], even_terms[g][:, t, chunk], ident[:], start=True, stop=False, is_transpose=True)
                    nc.tensor.matmul(sums[:, c, t, :], odd_terms[g][:, t, chunk], ident[:], start=False, stop=True, is_transpose=True)
            rounded = sb.tile([P, 2, P, 2], BF16, name="rounded%d" % g)
            nc.scalar.copy(rounded[:], sums[:].rearrange("s c t p -> s c p t"))
            rounded_words = rounded[:].rearrange("s c p t -> s (c p t)").bitcast(F32)
            for c in range(2):
                chunk = slice(c * P, (c + 1) * P)
                nc.tensor.transpose(turned_back[:, g, chunk], rounded_words[:, chunk], ident[:])
        for g in range(2):
            nc.scalar.copy(pairs[g][:, 0, :], turned_back[:, g, :])

        even_terms, odd_terms = second_pair_terms(0), second_pair_terms(1)
        for g in range(2):
            nc.vector.tensor_tensor(pairs[g][:, 1, :].bitcast(BF16), even_terms[g][:].rearrange("p s t -> p (s t)"),
                                    odd_terms[g][:].rearrange("p s t -> p (s t)"), ALU.add)

        q_grouped = sb.tile([P, QB, P, PACK], BF16, name="q_grouped", align_bytes=64)
        nc.scalar.copy(q_grouped[:], q_raw[:].rearrange("p t (m b) -> p b m t", b=QB))
        neg_lse = sb.tile([P, QB], F32, name="neg_lse")
        nc.scalar.mul(neg_lse[:], lse[:], -1.0)
        q_codes, q_scales = quantize("q", q_grouped[:].rearrange("p b m t -> p (b m t)"))

        u = [sb.tile([P, HALF, 2], F32, name="u%d" % g, align_bytes=64) for g in range(2)]
        for g, copy in enumerate((nc.scalar.copy, nc.vector.tensor_copy)):
            copy(u[g][:], pairs[g][:].rearrange("p h s -> p s h"))
        u_mx = [quantize("u%d" % g, u[g][:].rearrange("p s h -> p (s h)").bitcast(BF16)) for g in range(2)]

        first_half = ps.tile([P, QB, HALF], F32, name="first_half", **SUMS)
        second_half = [ps.tile([P, HALF], F32, name="second_half%d" % b, **ring) for b, ring in enumerate((SUMS, VALUE_TURNS))]
        scores = [[first_half[:, b, :] for b in range(QB)], [second_half[b][:] for b in range(QB)]]
        e = [sb.tile([P, PACK, P], F32, name="e%d" % b) for b in range(QB)]
        for g in range(2):
            u_codes, u_scales = u_mx[g]
            for b in range(QB):
                cols = slice(b * P, (b + 1) * P)
                nc.tensor.matmul_mx(scores[g][b], q_codes[:, cols].bitcast(FP8X4), q_scales[:, cols],
                                    u_codes.bitcast(FP8X4), u_scales, start=True, stop=True)
            for b in range(QB):
                nc.scalar.activation(e[b][:, :, g * HALF // PACK : (g + 1) * HALF // PACK],
                                     scores[g][b].rearrange("p (s r) -> p r s", r=PACK),
                                     ACT.Exp, bias=neg_lse[:, b : b + 1])

        y = sb.tile([P, QB, P, PACK], BF16, name="y", align_bytes=64)
        e_turned = []
        for b in range(QB):
            bank = ps.tile([P, PACK, P], F32, name="e_turned%d" % b, **TURNS)
            for r in range(PACK):
                nc.tensor.transpose(bank[:, r, :], e[b][:, r, :], ident[:])
            e_turned.append(bank)

        for b in range(QB):
            y_rows = sb.tile([P, PACK, P], BF16, name="y_rows%d" % b)
            for r in range(PACK):
                nc.scalar.activation(y_rows[:, r, :], e_turned[b][:, r, :], ACT.Copy, scale=slot_scale[:, r : r + 1])
            nc.scalar.copy(y[:, b].rearrange("p (c i) r -> p c r i", i=4), y_rows[:].rearrange("p r (c i) -> p c r i", i=4))

        def turn_values(j, grouped):
            gathered = sb.tile([P, N], BF16, name="gathered%d" % j, align_bytes=64)
            nc.vector.tensor_copy(gathered[:], values[j][:].indirect(tok_list[:]))
            words = gathered[:].bitcast(F32)
            bank = ps.tile([P, 2, P], F32, name="v_turned", **VALUE_TURNS)
            for h in range(2):
                nc.tensor.transpose(bank[:, h, :], words[:, h : N // 2 : 2], ident[:])
            nc.scalar.copy(grouped.rearrange("p (e h) -> p e h", h=2), bank[:].rearrange("p h e -> p e h"))

        out_rows = out[0].rearrange("(m b) e -> m b e", b=QB)
        results = [sb.tile([P, QB, DV // 2], F32, name="result%d" % i) for i in range(2)]

        def multiply(result, v_mx, ring):
            v_codes, v_scales = v_mx
            for b, copy in enumerate((nc.vector.tensor_copy, nc.scalar.copy)):
                cols = slice(b * P, (b + 1) * P)
                acc = ps.tile([P, result.shape[2]], F32, name="acc", **ring)
                nc.tensor.matmul_mx(acc[:], y_codes[:, cols].bitcast(FP8X4), y_scales[:, cols],
                                    v_codes.bitcast(FP8X4), v_scales, start=True, stop=True)
                copy(result[:, b, :], acc[:])

        plane_words = 2 * P
        v01 = sb.tile([P, 2 * plane_words], F32, name="v01", align_bytes=64)
        v2 = sb.tile([P, plane_words], F32, name="v2", align_bytes=64)
        v3 = sb.tile([P, plane_words], F32, name="v3", align_bytes=64)
        turn_values(0, v01[:, 0:plane_words])
        turn_values(1, v01[:, plane_words : 2 * plane_words])
        turn_values(2, v2[:])
        turn_values(3, v3[:])

        late_codes = sb.tile([P, NQ + 3 * P], U32, name="late_codes", tag="value3", align_bytes=64)
        y_codes, y_scales = quantize_into(late_codes[:, 0:NQ], "y", y[:].rearrange("p b q r -> p (b q r)"))
        v01_mx = quantize_into(late_codes[:, NQ : NQ + 2 * P], "v01", v01[:].bitcast(BF16))
        v2_mx = quantize_into(late_codes[:, NQ + 2 * P : NQ + 3 * P], "v2", v2[:].bitcast(BF16))
        v3_mx = quantize("v3", v3[:].bitcast(BF16))

        multiply(results[0][:], v01_mx, SUMS)
        nc.sync.dma_start(out=out_rows[:, :, 0 : DV // 2], in_=results[0][:])
        multiply(results[1][:, :, 0:P], v2_mx, TURNS)
        multiply(results[1][:, :, P : 2 * P], v3_mx, VALUE_TURNS)
        nc.sync.dma_start(out=out_rows[:, :, DV // 2 : DV], in_=results[1][:])
